import numpy as np
import ml_dtypes


def mxq(x, axis, fmt="e4m3"):
    dtype, down = {"e4m3": (ml_dtypes.float8_e4m3fn, 7), "e5m2": (ml_dtypes.float8_e5m2, 14)}[fmt]
    v = np.moveaxis(np.asarray(x, np.float32).astype(ml_dtypes.bfloat16).astype(np.float64), axis, -1)
    blocks = v.reshape(v.shape[:-1] + (-1, 32))
    amax = np.abs(blocks).max(-1, keepdims=True)
    byte = np.maximum(np.where(amax > 0, np.frexp(amax)[1] - 1 + 127, 0) - down, 1)
    scale = np.exp2(byte - 127.0)
    codes = (blocks / scale).astype(np.float32).astype(dtype).astype(np.float64)
    return np.moveaxis((codes * scale).reshape(v.shape), -1, axis)


WIDE = False


def mx_kscale(k):
    if not WIDE:
        return np.ones(k)
    levels = np.array([10, -10, 5, -5, 0])
    if k % 512:
        return np.exp2(np.random.permutation(np.resize(levels, k // 32))).repeat(32)
    a = np.empty((k // 512, 16))
    for p in range(k // 512):
        a[p, :8] = np.random.permutation(np.resize(levels, 8))
        for g in range(8):
            far = levels[np.abs(levels - a[p, g]) >= 10]
            a[p, g + 8] = far[np.random.randint(len(far))]
    return np.exp2(a.ravel()).repeat(32)


def f64(x):
    return np.asarray(x).astype(np.float64)


def striped(idx):
    return np.tile(np.asarray(idx).reshape(-1, 16).T, (8, 1)).astype(np.uint16)


def unstriped(offs):
    return offs[:16].T.reshape(-1).astype(np.int64)


E2M1 = np.array([0.0, 0.5, 1.0, 1.5, 2.0, 3.0, 4.0, 6.0, -0.0, -0.5, -1.0, -1.5, -2.0, -3.0, -4.0, -6.0])


def pack_weight(w, fmt):
    k, n = w.shape
    w = f64(np.asarray(w, np.float32).astype(ml_dtypes.bfloat16)).reshape(k // 32, 32, n)
    amax = np.abs(w).max(1)
    if fmt == "e4m3":
        byte = np.frexp(amax)[1] - 1 + 127 - 7
    else:
        mant, ex = np.frexp(amax / 6.0)
        byte = np.where(mant > 0.5, ex, ex - 1) + 127
    byte = np.clip(np.where(amax > 0, byte, 1), 1, 254)
    scaled = (w * np.exp2(127.0 - byte)[:, None, :]).reshape(k, n).astype(np.float32)
    by_word = np.ascontiguousarray(scaled.reshape(k // 512, 128, 4, n).transpose(0, 1, 3, 2))
    if fmt == "e4m3":
        words = by_word.astype(ml_dtypes.float8_e4m3fn).view(np.uint8)
    else:
        c = by_word.astype(ml_dtypes.float4_e2m1fn).view(np.uint8) & 0xF
        words = (c[..., 0::2] | (c[..., 1::2] << 4)).reshape(k // 512, 128, 2 * n)
    return np.ascontiguousarray(words), np.ascontiguousarray(byte.astype(np.uint8).reshape(k // 512, 16, n))


def unpack_weight(words, scales, fmt):
    g, _, n = scales.shape
    words = np.ascontiguousarray(words).reshape(g, 128, n, -1)
    if fmt == "e4m3":
        vals = words.view(ml_dtypes.float8_e4m3fn).astype(np.float64)
    else:
        nib = np.empty((g, 128, n, 4), np.uint8)
        nib[..., 0::2] = words & 0xF
        nib[..., 1::2] = words >> 4
        vals = E2M1[nib]
    vals = vals * np.repeat(np.exp2(scales.astype(np.float64) - 127.0), 8, axis=1)[..., None]
    return vals.transpose(0, 1, 3, 2).reshape(g * 512, n)


def e4m3fn_bytes(y):
    return np.clip(np.asarray(y, np.float64), -448.0, 448.0).astype(np.float32).astype(ml_dtypes.float8_e4m3fn).view(np.uint8)


def e4m3fn_values(b):
    return np.asarray(b, np.uint8).view(ml_dtypes.float8_e4m3fn).astype(np.float64)


K, V, J, N, E = 512, 1024, 256, 256, 512


def setup_inputs():
    n = np.random.standard_normal
    idx = np.random.permutation(V)[:J]
    idx2 = np.random.permutation(V)[:J]
    idx3 = np.random.permutation(E)[:J]
    fk = mx_kscale(K)
    wp = pack_weight(n((K, N)) * 1 / np.sqrt(K) / fk[:, None], "e2m1")
    w2p = pack_weight(n((K, N)) * 1 / np.sqrt(K) / fk[:, None], "e2m1")
    return {
        "ca": e4m3fn_bytes(60.0 * n((K, V))),
        "sa": (np.random.uniform(0.004, 0.012, (K, 1)) * fk[:, None]).astype(np.float32),
        "sb": (np.random.uniform(0.004, 0.012, (K, 1)) * fk[:, None]).astype(np.float32),
        "w_words": wp[0],
        "w_scales": wp[1],
        "w2_words": w2p[0],
        "w2_scales": w2p[1],
        "so": (np.random.uniform(0.5, 1.6, (N, 1))).astype(np.float32),
        "offs": striped(idx),
        "offs2": striped(idx2),
        "offs3": striped(idx3),
    }


def reference(ca, sa, sb, w_words, w_scales, w2_words, w2_scales, so, offs, offs2, offs3):
    idx = unstriped(offs)
    idx2 = unstriped(offs2)
    idx3 = unstriped(offs3)
    wu = unpack_weight(w_words, w_scales, "e2m1")
    w2u = unpack_weight(w2_words, w2_scales, "e2m1")
    z1 = np.maximum(e4m3fn_values(ca)[:, idx], e4m3fn_values(ca)[:, idx2]) * f64(sa)
    z2 = np.minimum(e4m3fn_values(ca)[:, idx], e4m3fn_values(ca)[:, idx2]) * f64(sb)
    z1q = mxq(z1, 0, "e4m3")
    z2q = mxq(z2, 0, "e4m3")
    p = wu.T @ z1q + w2u.T @ z2q
    y = np.zeros((N, E))
    y[:, idx3] = p * f64(so)
    return y

@@ -1,0 +1,115 @@
+from contextlib import ExitStack
+
+import concourse.mybir as mybir
+
+K, V, J, N, E = 512, 1024, 256, 256, 512
+FLOPS = 2 * 2 * K * N * J
+
+F32 = mybir.dt.float32
+BF16 = mybir.dt.bfloat16
+I32 = mybir.dt.int32
+U32 = mybir.dt.uint32
+U16 = mybir.dt.uint16
+U8 = mybir.dt.uint8
+FP8 = mybir.dt.float8_e4m3fn
+FP8X4 = mybir.dt.float8_e4m3fn_x4
+FP4X4 = mybir.dt.float4_e2m1fn_x4
+ALU = mybir.AluOpType
+ACT = mybir.ActivationFunctionType
+
+P = 128
+PACK = 4
+HALF = 128
+
+
+def tile_list_sortedpair_kernel(tc, ca, sa, sb, w_words, w_scales, w2_words, w2_scales, so, offs, offs2, offs3, out):
+    nc = tc.nc
+    with ExitStack() as ctx:
+        keep = ctx.enter_context(tc.tile_pool(name="keep", bufs=1))
+        psum = ctx.enter_context(tc.psum_pool(name="psum", bufs=1))
+
+        lists = [keep.tile([P, J // 16], U16, name="list%d" % i) for i in range(3)]
+        table = [keep.tile([P, V], U8, name="table%d" % t) for t in range(PACK)]
+        steps = [keep.tile([P, PACK], F32, name="steps%d" % z) for z in range(2)]
+        gains = keep.tile([P, N // P], F32)
+        words = [keep.tile([P, 2 * N], U8, name="words%d" % z, align_bytes=64) for z in range(2)]
+        planes = [keep.tile([P, N], U8, name="planes%d" % z, align_bytes=64) for z in range(2)]
+        pages = [keep.tile([P, E], F32, name="page%d" % n) for n in range(N // P)]
+
+        for z in range(2):
+            nc.gpsimd.memset(planes[z][:].bitcast(I32), 0)
+        for n in range(N // P):
+            nc.gpsimd.memset(pages[n][:], 0.0)
+
+        rows = ca.rearrange("(p t) v -> t p v", t=PACK)
+        nc.sync.dma_start(lists[0][:], offs)
+        nc.sync.dma_start(out=table[0][:], in_=rows[0])
+        nc.sync.dma_start(lists[1][:], offs2)
+        for t in range(1, PACK):
+            nc.sync.dma_start(out=table[t][:], in_=rows[t])
+        for z, s in enumerate((sa, sb)):
+            nc.sync.dma_start(out=steps[z][:], in_=s.rearrange("(p t) o -> p (t o)", t=PACK))
+        for z, (ww, ws) in enumerate(((w_words, w_scales), (w2_words, w2_scales))):
+            nc.sync.dma_start(out=words[z][:], in_=ww[0])
+            for q in range(4):
+                nc.sync.dma_start(
+                    out=planes[z][32 * q : 32 * q + 4, :].bitcast(I32),
+                    in_=ws[0, 4 * q : 4 * q + 4, :].bitcast(I32),
+                )
+        nc.sync.dma_start(lists[2][:], offs3)
+        with nc.allow_non_contiguous_dma(reason="one weight a partition"):
+            nc.sync.dma_start(out=gains[:], in_=so.rearrange("(h p) o -> p (h o)", p=P))
+
+        picked = [[keep.tile([P, J], U8, name="picked%d_%d" % (i, t)) for t in range(PACK)] for i in range(2)]
+        value = [keep.tile([P, PACK, J], F32, name="value%d" % i) for i in range(2)]
+        for t in range(PACK):
+            for i in range(2):
+                nc.vector.tensor_copy(picked[i][t][:], table[t][:].indirect(lists[i][:]))
+                nc.scalar.copy(value[i][:, t, :], picked[i][t][:].bitcast(FP8))
+
+        for h in range(J // HALF):
+            cols = slice(h * HALF, (h + 1) * HALF)
+            ends = [keep.tile([P, PACK, HALF], F32, name="ends%d_%d" % (h, z)) for z in range(2)]
+            groups = (slice(0, PACK - 1), slice(PACK - 1, PACK)) if h == 0 else (slice(0, PACK),)
+            for ts in groups:
+                for z, op in enumerate((ALU.max, ALU.min)):
+                    nc.vector.tensor_tensor(ends[z][:, ts, :], value[0][:, ts, cols], value[1][:, ts, cols], op)
+            woven = [keep.tile([P, HALF * PACK], BF16, name="woven%d_%d" % (h, z), align_bytes=64) for z in range(2)]
+            codes = [keep.tile([P, HALF], U32, name="code%d_%d" % (h, z), align_bytes=64) for z in range(2)]
+            scales = [keep.tile([P, HALF], U8, name="scale%d_%d" % (h, z), align_bytes=64) for z in range(2)]
+            for z in range(2):
+                nc.vector.tensor_tensor(
+                    woven[z][:].rearrange("p (c i t) -> p c t i", i=2, t=PACK),
+                    ends[z][:].rearrange("p t (c i) -> p c t i", i=2),
+                    steps[z][:].unsqueeze(1).unsqueeze(3).to_broadcast([P, HALF // 2, PACK, 2]),
+                    ALU.mult,
+                )
+            for z in range(2):
+                nc.vector.quantize_mx(out=codes[z][:].bitcast(FP8X4), scales=scales[z][:], in_=woven[z][:])
+            sums = [psum.tile([P, HALF], F32, name="sums%d_%d" % (h, n)) for n in range(N // P)]
+            for z in range(2):
+                for n in range(N // P):
+                    nc.tensor.matmul_mx(
+                        out=sums[n][:],
+                        lhsT=words[z][:, 2 * P * n : 2 * P * (n + 1)].bitcast(FP4X4),
+                        lhsT_scale=planes[z][:, P * n : P * (n + 1)],
+                        rhs=codes[z][:].bitcast(FP8X4),
+                        rhs_scale=scales[z][:],
+                        start=(z == 0),
+                        stop=(z == 1),
+                    )
+            prods = [keep.tile([P, HALF], F32, name="prod%d_%d" % (h, n)) for n in range(N // P)]
+            for n in range(N // P):
+                if h == 0:
+                    nc.scalar.copy(prods[n][:], sums[n][:])
+                else:
+                    nc.vector.tensor_copy(prods[n][:], sums[n][:])
+            for n in range(N // P):
+                nc.scalar.activation(
+                    out=pages[n][:].indirect(lists[2][:, 8 * h : 8 * (h + 1)]),
+                    in_=prods[n][:],
+                    func=ACT.Copy,
+                    scale=gains[:, n : n + 1],
+                )
+        for n in range(N // P):
+            nc.sync.dma_start(out=out[P * n : P * (n + 1), :], in_=pages[n][:])

@@ -60,50 +60,36 @@ def tile_list_sortedpair_kernel(tc, ca, sa, sb, w_words, w_scales, w2_words, w2_
         with nc.allow_non_contiguous_dma(reason="one weight a partition"):
             nc.sync.dma_start(out=gains[:], in_=so.rearrange("(h p) o -> p (h o)", p=P))
 
-        picked = [[keep.tile([P, J], U8, name="picked%d_%d" % (i, t)) for t in range(PACK)] for i in range(2)]
-        value = [keep.tile([P, PACK, J], F32, name="value%d" % i) for i in range(2)]
-        for t in range(PACK):
+        def look_up(part, t, dst):
             for i in range(2):
-                nc.vector.tensor_copy(picked[i][t][:], table[t][:].indirect(lists[i][:]))
-                nc.scalar.copy(value[i][:, t, :], picked[i][t][:].bitcast(FP8))
+                nc.vector.tensor_copy(dst[:, i, :], table[t][:].indirect(lists[i][:, part]))
 
-        for h in range(J // HALF):
-            cols = slice(h * HALF, (h + 1) * HALF)
-            ends = [keep.tile([P, PACK, HALF], F32, name="ends%d_%d" % (h, z)) for z in range(2)]
-            groups = (slice(0, PACK - 1), slice(PACK - 1, PACK)) if h == 0 else (slice(0, PACK),)
-            for ts in groups:
-                for z, op in enumerate((ALU.max, ALU.min)):
-                    nc.vector.tensor_tensor(ends[z][:, ts, :], value[0][:, ts, cols], value[1][:, ts, cols], op)
-            woven = [keep.tile([P, HALF * PACK], BF16, name="woven%d_%d" % (h, z), align_bytes=64) for z in range(2)]
-            codes = [keep.tile([P, HALF], U32, name="code%d_%d" % (h, z), align_bytes=64) for z in range(2)]
-            scales = [keep.tile([P, HALF], U8, name="scale%d_%d" % (h, z), align_bytes=64) for z in range(2)]
-            for z in range(2):
-                nc.vector.tensor_tensor(
-                    woven[z][:].rearrange("p (c i t) -> p c t i", i=2, t=PACK),
-                    ends[z][:].rearrange("p t (c i) -> p c t i", i=2),
-                    steps[z][:].unsqueeze(1).unsqueeze(3).to_broadcast([P, HALF // 2, PACK, 2]),
-                    ALU.mult,
-                )
-            for z in range(2):
-                nc.vector.quantize_mx(out=codes[z][:].bitcast(FP8X4), scales=scales[z][:], in_=woven[z][:])
-            sums = [psum.tile([P, HALF], F32, name="sums%d_%d" % (h, n)) for n in range(N // P)]
+        def read(src, dst):
+            nc.scalar.copy(dst.rearrange("p i j -> p (i j)"), src.rearrange("p i j -> p (i j)").bitcast(FP8))
+
+        def sort_pair(first, second, dsts):
+            for op, dst in zip((ALU.max, ALU.min), dsts):
+                nc.vector.tensor_tensor(dst, first, second, op)
+
+        def multiply(h, codes, scales):
+            sums = [psum.tile([P, HALF], F32, name="sums%d_%d" % (h, n), tag="sums%d" % n) for n in range(N // P)]
             for z in range(2):
                 for n in range(N // P):
                     nc.tensor.matmul_mx(
                         out=sums[n][:],
                         lhsT=words[z][:, 2 * P * n : 2 * P * (n + 1)].bitcast(FP4X4),
                         lhsT_scale=planes[z][:, P * n : P * (n + 1)],
-                        rhs=codes[z][:].bitcast(FP8X4),
-                        rhs_scale=scales[z][:],
+                        rhs=codes[z].bitcast(FP8X4),
+                        rhs_scale=scales[z],
                         start=(z == 0),
                         stop=(z == 1),
                     )
+            return sums
+
+        def put(h, sums, copy):
             prods = [keep.tile([P, HALF], F32, name="prod%d_%d" % (h, n)) for n in range(N // P)]
             for n in range(N // P):
-                if h == 0:
-                    nc.scalar.copy(prods[n][:], sums[n][:])
-                else:
-                    nc.vector.tensor_copy(prods[n][:], sums[n][:])
+                copy(prods[n][:], sums[n][:])
             for n in range(N // P):
                 nc.scalar.activation(
                     out=pages[n][:].indirect(lists[2][:, 8 * h : 8 * (h + 1)]),
@@ -111,5 +97,66 @@ def tile_list_sortedpair_kernel(tc, ca, sa, sb, w_words, w_scales, w2_words, w2_
                     func=ACT.Copy,
                     scale=gains[:, n : n + 1],
                 )
+
+        work = keep.tile([P, 16, HALF], F32, align_bytes=64)
+        ends = [[work[:, 0:4, :], work[:, 4:8, :]], [work[:, 6:10, :], work[:, 12:16, :]]]
+        pairs = work[:, 8:12, :].rearrange("p (z u) j -> p z u j", z=2)
+        woven = work[:, 12:16, :].rearrange("p s j -> p (s j)")
+
+        def scale_pair(u):
+            for z in range(2):
+                for e in range(2):
+                    t = 2 * u + e
+                    nc.scalar.activation(
+                        out=pairs[:, z, u, :].bitcast(BF16)[:, e : 2 * HALF : 2], in_=ends[0][z][:, t, :], func=ACT.Copy, scale=steps[z][:, t : t + 1]
+                    )
+
+        low = keep.tile([P, 2, 2, J], F32)
+        high = [keep.tile([P, 2, 2, HALF], F32, name="high%d" % h) for h in range(2)]
+        for t in range(2):
+            picked = keep.tile([P, 2, J], U8, name="picked_%d" % t)
+            look_up(slice(0, J // 16), t, picked)
+            read(picked[:], low[:, t])
+        for e in range(2):
+            picked = keep.tile([P, 2, HALF], U8, name="picked0_%d" % e, tag="late%d" % e)
+            look_up(slice(0, 8), 2 + e, picked)
+            read(picked[:], high[0][:, e])
+        sort_pair(low[:, :, 0, 0:HALF], low[:, :, 1, 0:HALF], [ends[0][z][:, 0:2, :] for z in range(2)])
+        sort_pair(high[0][:, :, 0, :], high[0][:, :, 1, :], [ends[0][z][:, 2:4, :] for z in range(2)])
+        scale_pair(0)
+        scale_pair(1)
+        picked = keep.tile([P, 2, 2, HALF], U8, name="picked1", tag="late1")
+        for e in range(2):
+            look_up(slice(8, 16), 2 + e, picked[:, e])
+            read(picked[:, e], high[1][:, e])
+
+        nc.vector.tensor_copy(
+            woven.rearrange("p (z c i u) -> p z c u i", z=2, i=2, u=2),
+            pairs.rearrange("p z u (c i) -> p z c u i", i=2),
+        )
+        codes = keep.tile([P, 2 * HALF], U32, name="codes0", align_bytes=64)
+        scales = keep.tile([P, 2 * HALF], U8, name="scales0", align_bytes=64)
+        nc.vector.quantize_mx(out=codes[:].bitcast(FP8X4), scales=scales[:], in_=woven.bitcast(BF16))
+        sums0 = multiply(
+            0, [codes[:, z * HALF : (z + 1) * HALF] for z in range(2)], [scales[:, z * HALF : (z + 1) * HALF] for z in range(2)]
+        )
+
+        sort_pair(low[:, :, 0, HALF:J], low[:, :, 1, HALF:J], [ends[1][z][:, 0:2, :] for z in range(2)])
+        sort_pair(high[1][:, :, 0, :], high[1][:, :, 1, :], [ends[1][z][:, 2:4, :] for z in range(2)])
+        woven1 = [keep.tile([P, HALF * PACK], BF16, name="woven1_%d" % z, align_bytes=64) for z in range(2)]
+        codes1 = [keep.tile([P, HALF], U32, name="codes1_%d" % z, align_bytes=64) for z in range(2)]
+        scales1 = [keep.tile([P, HALF], U8, name="scales1_%d" % z, align_bytes=64) for z in range(2)]
+        for z in range(2):
+            nc.vector.tensor_tensor(
+                woven1[z][:].rearrange("p (c i t) -> p c t i", i=2, t=PACK),
+                ends[1][z].rearrange("p t (c i) -> p c t i", i=2),
+                steps[z][:].unsqueeze(1).unsqueeze(3).to_broadcast([P, HALF // 2, PACK, 2]),
+                ALU.mult,
+            )
+        for z in range(2):
+            nc.vector.quantize_mx(out=codes1[z][:].bitcast(FP8X4), scales=scales1[z][:], in_=woven1[z][:])
+        put(0, sums0, nc.scalar.copy)
+        sums1 = multiply(1, [codes1[z][:] for z in range(2)], [scales1[z][:] for z in range(2)])
+        put(1, sums1, nc.vector.tensor_copy)
         for n in range(N // P):
             nc.sync.dma_start(out=out[P * n : P * (n + 1), :], in_=pages[n][:])

@@ -42,8 +42,8 @@ def tile_list_sortedpair_kernel(tc, ca, sa, sb, w_words, w_scales, w2_words, w2_
             nc.gpsimd.memset(pages[n][:], 0.0)
 
         rows = ca.rearrange("(p t) v -> t p v", t=PACK)
-        nc.sync.dma_start(lists[0][:], offs)
         nc.sync.dma_start(out=table[0][:], in_=rows[0])
+        nc.sync.dma_start(lists[0][:], offs)
         nc.sync.dma_start(lists[1][:], offs2)
         for t in range(1, PACK):
             nc.sync.dma_start(out=table[t][:], in_=rows[t])
@@ -73,8 +73,9 @@ def tile_list_sortedpair_kernel(tc, ca, sa, sb, w_words, w_scales, w2_words, w2_
 
         def multiply(h, codes, scales):
             sums = [psum.tile([P, HALF], F32, name="sums%d_%d" % (h, n), tag="sums%d" % n) for n in range(N // P)]
-            for z in range(2):
-                for n in range(N // P):
+            order = [(z, n) for n in range(2) for z in range(2)] if h == 0 else [(z, n) for z in range(2) for n in range(2)]
+            for z, n in order:
+                if True:
                     nc.tensor.matmul_mx(
                         out=sums[n][:],
                         lhsT=words[z][:, 2 * P * n : 2 * P * (n + 1)].bitcast(FP4X4),
@@ -98,58 +99,59 @@ def tile_list_sortedpair_kernel(tc, ca, sa, sb, w_words, w_scales, w2_words, w2_
                     scale=gains[:, n : n + 1],
                 )
 
-        work = keep.tile([P, 16, HALF], F32, align_bytes=64)
-        ends = [[work[:, 0:4, :], work[:, 4:8, :]], [work[:, 6:10, :], work[:, 12:16, :]]]
-        pairs = work[:, 8:12, :].rearrange("p (z u) j -> p z u j", z=2)
-        woven = work[:, 12:16, :].rearrange("p s j -> p (s j)")
-
-        def scale_pair(u):
+        parts = [slice(0, 8), slice(8, 16)]
+        value0 = keep.tile([P, PACK, 2, HALF], F32)
+        for t in range(PACK):
+            picked = keep.tile([P, 2, HALF], U8, name="picked0_%d" % t, tag="picked%d" % t)
+            look_up(parts[0], t, picked)
+            read(picked[:], value0[:, t])
+        ends0 = [
+            [keep.tile([P, 2, HALF], F32, name="ends0_%d_%d" % (z, u), tag="ends0_%d_%d" % (z, u)) for u in range(2)]
+            for z in range(2)
+        ]
+        pairs = keep.tile([P, 2, 2, HALF, 2], BF16, name="pairs", tag="pairs")
+        for u in range(2):
+            ts = slice(2 * u, 2 * u + 2)
+            sort_pair(value0[:, ts, 0, :], value0[:, ts, 1, :], [ends0[z][u][:] for z in range(2)])
+        for u in range(2):
             for z in range(2):
                 for e in range(2):
                     t = 2 * u + e
                     nc.scalar.activation(
-                        out=pairs[:, z, u, :].bitcast(BF16)[:, e : 2 * HALF : 2], in_=ends[0][z][:, t, :], func=ACT.Copy, scale=steps[z][:, t : t + 1]
+                        out=pairs[:, z, u, :, e], in_=ends0[z][u][:, e, :], func=ACT.Copy, scale=steps[z][:, t : t + 1]
                     )
-
-        low = keep.tile([P, 2, 2, J], F32)
-        high = [keep.tile([P, 2, 2, HALF], F32, name="high%d" % h) for h in range(2)]
-        for t in range(2):
-            picked = keep.tile([P, 2, J], U8, name="picked_%d" % t)
-            look_up(slice(0, J // 16), t, picked)
-            read(picked[:], low[:, t])
-        for e in range(2):
-            picked = keep.tile([P, 2, HALF], U8, name="picked0_%d" % e, tag="late%d" % e)
-            look_up(slice(0, 8), 2 + e, picked)
-            read(picked[:], high[0][:, e])
-        sort_pair(low[:, :, 0, 0:HALF], low[:, :, 1, 0:HALF], [ends[0][z][:, 0:2, :] for z in range(2)])
-        sort_pair(high[0][:, :, 0, :], high[0][:, :, 1, :], [ends[0][z][:, 2:4, :] for z in range(2)])
-        scale_pair(0)
-        scale_pair(1)
-        picked = keep.tile([P, 2, 2, HALF], U8, name="picked1", tag="late1")
-        for e in range(2):
-            look_up(slice(8, 16), 2 + e, picked[:, e])
-            read(picked[:, e], high[1][:, e])
-
-        nc.vector.tensor_copy(
-            woven.rearrange("p (z c i u) -> p z c u i", z=2, i=2, u=2),
-            pairs.rearrange("p z u (c i) -> p z c u i", i=2),
+        woven = keep.tile([P, 2 * HALF * 2], F32, name="woven0", align_bytes=64)
+        nc.scalar.copy(
+            woven[:].rearrange("p (z c i u) -> p z c u i", z=2, i=2, u=2),
+            pairs[:].rearrange("p z u j e -> p z u (j e)").bitcast(F32).rearrange("p z u (c i) -> p z c u i", i=2),
         )
+
+        head = keep.tile([P, 2, HALF], U8, name="picked1_0", tag="picked2")
+        rest = keep.tile([P, PACK - 1, 2, HALF], U8, name="picked1_rest", tag="ends0_0_0")
+        value1 = keep.tile([P, PACK, 2, HALF], F32, name="value1", tag="pairs")
+        for t in range(PACK):
+            picked = head[:] if t == 0 else rest[:, t - 1]
+            look_up(parts[1], t, picked)
+            read(picked, value1[:, t])
+
         codes = keep.tile([P, 2 * HALF], U32, name="codes0", align_bytes=64)
         scales = keep.tile([P, 2 * HALF], U8, name="scales0", align_bytes=64)
-        nc.vector.quantize_mx(out=codes[:].bitcast(FP8X4), scales=scales[:], in_=woven.bitcast(BF16))
+        nc.vector.quantize_mx(out=codes[:].bitcast(FP8X4), scales=scales[:], in_=woven[:].bitcast(BF16))
         sums0 = multiply(
             0, [codes[:, z * HALF : (z + 1) * HALF] for z in range(2)], [scales[:, z * HALF : (z + 1) * HALF] for z in range(2)]
         )
 
-        sort_pair(low[:, :, 0, HALF:J], low[:, :, 1, HALF:J], [ends[1][z][:, 0:2, :] for z in range(2)])
-        sort_pair(high[1][:, :, 0, :], high[1][:, :, 1, :], [ends[1][z][:, 2:4, :] for z in range(2)])
+        ends1 = [keep.tile([P, PACK, HALF], F32, name="ends1_%d" % z) for z in range(2)]
+        for u in range(2):
+            ts = slice(2 * u, 2 * u + 2)
+            sort_pair(value1[:, ts, 0, :], value1[:, ts, 1, :], [ends1[z][:, ts, :] for z in range(2)])
         woven1 = [keep.tile([P, HALF * PACK], BF16, name="woven1_%d" % z, align_bytes=64) for z in range(2)]
         codes1 = [keep.tile([P, HALF], U32, name="codes1_%d" % z, align_bytes=64) for z in range(2)]
         scales1 = [keep.tile([P, HALF], U8, name="scales1_%d" % z, align_bytes=64) for z in range(2)]
         for z in range(2):
             nc.vector.tensor_tensor(
                 woven1[z][:].rearrange("p (c i t) -> p c t i", i=2, t=PACK),
-                ends[1][z].rearrange("p t (c i) -> p c t i", i=2),
+                ends1[z][:].rearrange("p t (c i) -> p c t i", i=2),
                 steps[z][:].unsqueeze(1).unsqueeze(3).to_broadcast([P, HALF // 2, PACK, 2]),
                 ALU.mult,
             )

from contextlib import ExitStack

import concourse.mybir as mybir

K, V, J, N, E = 512, 1024, 256, 256, 512
FLOPS = 2 * 2 * K * N * J

F32 = mybir.dt.float32
BF16 = mybir.dt.bfloat16
I32 = mybir.dt.int32
U32 = mybir.dt.uint32
U16 = mybir.dt.uint16
U8 = mybir.dt.uint8
FP8 = mybir.dt.float8_e4m3fn
FP8X4 = mybir.dt.float8_e4m3fn_x4
FP4X4 = mybir.dt.float4_e2m1fn_x4
ALU = mybir.AluOpType
ACT = mybir.ActivationFunctionType

P = 128
PACK = 4
HALF = 128


def tile_list_sortedpair_kernel(tc, ca, sa, sb, w_words, w_scales, w2_words, w2_scales, so, offs, offs2, offs3, out):
    nc = tc.nc
    with ExitStack() as ctx:
        keep = ctx.enter_context(tc.tile_pool(name="keep", bufs=1))
        psum = ctx.enter_context(tc.psum_pool(name="psum", bufs=1))

        lists = [keep.tile([P, J // 16], U16, name="list%d" % i) for i in range(3)]
        table = [keep.tile([P, V], U8, name="table%d" % t) for t in range(PACK)]
        steps = [keep.tile([P, PACK], F32, name="steps%d" % z) for z in range(2)]
        gains = keep.tile([P, N // P], F32)
        words = [keep.tile([P, 2 * N], U8, name="words%d" % z, align_bytes=64) for z in range(2)]
        planes = [keep.tile([P, N], U8, name="planes%d" % z, align_bytes=64) for z in range(2)]
        pages = [keep.tile([P, E], F32, name="page%d" % n) for n in range(N // P)]

        for z in range(2):
            nc.gpsimd.memset(planes[z][:].bitcast(I32), 0)
        for n in range(N // P):
            nc.gpsimd.memset(pages[n][:], 0.0)

        rows = ca.rearrange("(p t) v -> t p v", t=PACK)
        nc.sync.dma_start(out=table[0][:], in_=rows[0])
        nc.sync.dma_start(lists[0][:], offs)
        nc.sync.dma_start(lists[1][:], offs2)
        for t in range(1, PACK):
            nc.sync.dma_start(out=table[t][:], in_=rows[t])
        for z, s in enumerate((sa, sb)):
            nc.sync.dma_start(out=steps[z][:], in_=s.rearrange("(p t) o -> p (t o)", t=PACK))
        for z, (ww, ws) in enumerate(((w_words, w_scales), (w2_words, w2_scales))):
            nc.sync.dma_start(out=words[z][:], in_=ww[0])
            for q in range(4):
                nc.sync.dma_start(
                    out=planes[z][32 * q : 32 * q + 4, :].bitcast(I32),
                    in_=ws[0, 4 * q : 4 * q + 4, :].bitcast(I32),
                )
        nc.sync.dma_start(lists[2][:], offs3)
        with nc.allow_non_contiguous_dma(reason="one weight a partition"):
            nc.sync.dma_start(out=gains[:], in_=so.rearrange("(h p) o -> p (h o)", p=P))

        def look_up(part, t, dst):
            for i in range(2):
                nc.vector.tensor_copy(dst[:, i, :], table[t][:].indirect(lists[i][:, part]))

        def read(src, dst):
            nc.scalar.copy(dst.rearrange("p i j -> p (i j)"), src.rearrange("p i j -> p (i j)").bitcast(FP8))

        def sort_pair(first, second, dsts):
            for op, dst in zip((ALU.max, ALU.min), dsts):
                nc.vector.tensor_tensor(dst, first, second, op)

        def multiply(h, codes, scales):
            sums = [psum.tile([P, HALF], F32, name="sums%d_%d" % (h, n), tag="sums%d" % n) for n in range(N // P)]
            order = [(z, n) for n in range(2) for z in range(2)] if h == 0 else [(z, n) for z in range(2) for n in range(2)]
            for z, n in order:
                if True:
                    nc.tensor.matmul_mx(
                        out=sums[n][:],
                        lhsT=words[z][:, 2 * P * n : 2 * P * (n + 1)].bitcast(FP4X4),
                        lhsT_scale=planes[z][:, P * n : P * (n + 1)],
                        rhs=codes[z].bitcast(FP8X4),
                        rhs_scale=scales[z],
                        start=(z == 0),
                        stop=(z == 1),
                    )
            return sums

        def put(h, sums, copy):
            prods = [keep.tile([P, HALF], F32, name="prod%d_%d" % (h, n)) for n in range(N // P)]
            for n in range(N // P):
                copy(prods[n][:], sums[n][:])
            for n in range(N // P):
                nc.scalar.activation(
                    out=pages[n][:].indirect(lists[2][:, 8 * h : 8 * (h + 1)]),
                    in_=prods[n][:],
                    func=ACT.Copy,
                    scale=gains[:, n : n + 1],
                )

        parts = [slice(0, 8), slice(8, 16)]
        value0 = keep.tile([P, PACK, 2, HALF], F32)
        for t in range(PACK):
            picked = keep.tile([P, 2, HALF], U8, name="picked0_%d" % t, tag="picked%d" % t)
            look_up(parts[0], t, picked)
            read(picked[:], value0[:, t])
        ends0 = [
            [keep.tile([P, 2, HALF], F32, name="ends0_%d_%d" % (z, u), tag="ends0_%d_%d" % (z, u)) for u in range(2)]
            for z in range(2)
        ]
        pairs = keep.tile([P, 2, 2, HALF, 2], BF16, name="pairs", tag="pairs")
        for u in range(2):
            ts = slice(2 * u, 2 * u + 2)
            sort_pair(value0[:, ts, 0, :], value0[:, ts, 1, :], [ends0[z][u][:] for z in range(2)])
        for u in range(2):
            for z in range(2):
                for e in range(2):
                    t = 2 * u + e
                    nc.scalar.activation(
                        out=pairs[:, z, u, :, e], in_=ends0[z][u][:, e, :], func=ACT.Copy, scale=steps[z][:, t : t + 1]
                    )
        woven = keep.tile([P, 2 * HALF * 2], F32, name="woven0", align_bytes=64)
        nc.scalar.copy(
            woven[:].rearrange("p (z c i u) -> p z c u i", z=2, i=2, u=2),
            pairs[:].rearrange("p z u j e -> p z u (j e)").bitcast(F32).rearrange("p z u (c i) -> p z c u i", i=2),
        )

        head = keep.tile([P, 2, HALF], U8, name="picked1_0", tag="picked2")
        rest = keep.tile([P, PACK - 1, 2, HALF], U8, name="picked1_rest", tag="ends0_0_0")
        value1 = keep.tile([P, PACK, 2, HALF], F32, name="value1", tag="pairs")
        for t in range(PACK):
            picked = head[:] if t == 0 else rest[:, t - 1]
            look_up(parts[1], t, picked)
            read(picked, value1[:, t])

        codes = keep.tile([P, 2 * HALF], U32, name="codes0", align_bytes=64)
        scales = keep.tile([P, 2 * HALF], U8, name="scales0", align_bytes=64)
        nc.vector.quantize_mx(out=codes[:].bitcast(FP8X4), scales=scales[:], in_=woven[:].bitcast(BF16))
        sums0 = multiply(
            0, [codes[:, z * HALF : (z + 1) * HALF] for z in range(2)], [scales[:, z * HALF : (z + 1) * HALF] for z in range(2)]
        )

        ends1 = [keep.tile([P, PACK, HALF], F32, name="ends1_%d" % z) for z in range(2)]
        for u in range(2):
            ts = slice(2 * u, 2 * u + 2)
            sort_pair(value1[:, ts, 0, :], value1[:, ts, 1, :], [ends1[z][:, ts, :] for z in range(2)])
        woven1 = [keep.tile([P, HALF * PACK], BF16, name="woven1_%d" % z, align_bytes=64) for z in range(2)]
        codes1 = [keep.tile([P, HALF], U32, name="codes1_%d" % z, align_bytes=64) for z in range(2)]
        scales1 = [keep.tile([P, HALF], U8, name="scales1_%d" % z, align_bytes=64) for z in range(2)]
        for z in range(2):
            nc.vector.tensor_tensor(
                woven1[z][:].rearrange("p (c i t) -> p c t i", i=2, t=PACK),
                ends1[z][:].rearrange("p t (c i) -> p c t i", i=2),
                steps[z][:].unsqueeze(1).unsqueeze(3).to_broadcast([P, HALF // 2, PACK, 2]),
                ALU.mult,
            )
        for z in range(2):
            nc.vector.quantize_mx(out=codes1[z][:].bitcast(FP8X4), scales=scales1[z][:], in_=woven1[z][:])
        put(0, sums0, nc.scalar.copy)
        sums1 = multiply(1, [codes1[z][:] for z in range(2)], [scales1[z][:] for z in range(2)])
        put(1, sums1, nc.vector.tensor_copy)
        for n in range(N // P):
            nc.sync.dma_start(out=out[P * n : P * (n + 1), :], in_=pages[n][:])
